import numpy as np
import ml_dtypes


def mxq(x, axis, fmt="e4m3"):
    dtype, down = {"e4m3": (ml_dtypes.float8_e4m3fn, 7), "e5m2": (ml_dtypes.float8_e5m2, 14)}[fmt]
    v = np.moveaxis(np.asarray(x, np.float32).astype(ml_dtypes.bfloat16).astype(np.float64), axis, -1)
    blocks = v.reshape(v.shape[:-1] + (-1, 32))
    amax = np.abs(blocks).max(-1, keepdims=True)
    byte = np.maximum(np.where(amax > 0, np.frexp(amax)[1] - 1 + 127, 0) - down, 1)
    scale = np.exp2(byte - 127.0)
    codes = (blocks / scale).astype(np.float32).astype(dtype).astype(np.float64)
    return np.moveaxis((codes * scale).reshape(v.shape), -1, axis)


WIDE = False


def mx_kscale(k):
    if not WIDE:
        return np.ones(k)
    levels = np.array([10, -10, 5, -5, 0])
    if k % 512:
        return np.exp2(np.random.permutation(np.resize(levels, k // 32))).repeat(32)
    a = np.empty((k // 512, 16))
    for p in range(k // 512):
        a[p, :8] = np.random.permutation(np.resize(levels, 8))
        for g in range(8):
            far = levels[np.abs(levels - a[p, g]) >= 10]
            a[p, g + 8] = far[np.random.randint(len(far))]
    return np.exp2(a.ravel()).repeat(32)


def f64(x):
    return np.asarray(x).astype(np.float64)


def striped8(idx):
    return np.asarray(idx).reshape(8, -1, 16).transpose(0, 2, 1).reshape(128, -1).astype(np.uint16)


def unstriped8(offs):
    return offs.reshape(8, 16, -1).transpose(0, 2, 1).reshape(8, -1).astype(np.int64)


def pick8(x, idx, run):
    r = np.arange(len(x))
    return x[r[:, None], idx[r % (8 * run) // run]]


E2M1 = np.array([0.0, 0.5, 1.0, 1.5, 2.0, 3.0, 4.0, 6.0, -0.0, -0.5, -1.0, -1.5, -2.0, -3.0, -4.0, -6.0])


def pack_weight(w, fmt):
    k, n = w.shape
    w = f64(np.asarray(w, np.float32).astype(ml_dtypes.bfloat16)).reshape(k // 32, 32, n)
    amax = np.abs(w).max(1)
    if fmt == "e4m3":
        byte = np.frexp(amax)[1] - 1 + 127 - 7
    else:
        mant, ex = np.frexp(amax / 6.0)
        byte = np.where(mant > 0.5, ex, ex - 1) + 127
    byte = np.clip(np.where(amax > 0, byte, 1), 1, 254)
    scaled = (w * np.exp2(127.0 - byte)[:, None, :]).reshape(k, n).astype(np.float32)
    by_word = np.ascontiguousarray(scaled.reshape(k // 512, 128, 4, n).transpose(0, 1, 3, 2))
    if fmt == "e4m3":
        words = by_word.astype(ml_dtypes.float8_e4m3fn).view(np.uint8)
    else:
        c = by_word.astype(ml_dtypes.float4_e2m1fn).view(np.uint8) & 0xF
        words = (c[..., 0::2] | (c[..., 1::2] << 4)).reshape(k // 512, 128, 2 * n)
    return np.ascontiguousarray(words), np.ascontiguousarray(byte.astype(np.uint8).reshape(k // 512, 16, n))


def unpack_weight(words, scales, fmt):
    g, _, n = scales.shape
    words = np.ascontiguousarray(words).reshape(g, 128, n, -1)
    if fmt == "e4m3":
        vals = words.view(ml_dtypes.float8_e4m3fn).astype(np.float64)
    else:
        nib = np.empty((g, 128, n, 4), np.uint8)
        nib[..., 0::2] = words & 0xF
        nib[..., 1::2] = words >> 4
        vals = E2M1[nib]
    vals = vals * np.repeat(np.exp2(scales.astype(np.float64) - 127.0), 8, axis=1)[..., None]
    return vals.transpose(0, 1, 3, 2).reshape(g * 512, n)


D, T, I, Q = 512, 1024, 512, 128


def setup_inputs():
    n = np.random.standard_normal
    idx = np.stack([np.random.permutation(T)[:I] for _ in range(8)])
    idx2 = np.stack([np.random.permutation(T)[:I] for _ in range(8)])
    idx3 = np.stack([np.random.permutation(T)[:I] for _ in range(8)])
    fd = mx_kscale(D)
    keysp = pack_weight(n((D, T)) / fd[:, None], "e4m3")
    return {
        "query": (n((D, Q)) * 0.9 / np.sqrt(D) * fd[:, None]).astype(np.float32),
        "query2": (n((D, Q)) * 0.9 / np.sqrt(D) * fd[:, None]).astype(np.float32),
        "keys_words": keysp[0],
        "keys_scales": keysp[1],
        "lam": (np.random.uniform(0.8, 1.6, (Q, 1))).astype(np.float32),
        "old": (1.0 * n((Q, T))).astype(np.float32),
        "offs": striped8(idx),
        "offs2": striped8(idx2),
        "offs3": striped8(idx3),
    }


def reference(query, query2, keys_words, keys_scales, lam, old, offs, offs2, offs3):
    idx = unstriped8(offs)
    idx2 = unstriped8(offs2)
    idx3 = unstriped8(offs3)
    keysu = unpack_weight(keys_words, keys_scales, "e4m3")
    queryq = mxq(f64(query), 0, "e4m3")
    a = queryq.T @ keysu
    query2q = mxq(f64(query2), 0, "e4m3")
    b = query2q.T @ keysu
    w = np.log(np.exp(pick8(a, idx, 16)) + np.exp(pick8(b, idx2, 16))) * f64(lam)
    f1 = np.zeros((Q, T))
    f1[np.arange(Q)[:, None], idx3[np.arange(Q) % 128 // 16]] = w
    y = f64(old) + f1
    return y

@@ -1,0 +1,146 @@
+from contextlib import ExitStack
+
+import concourse.mybir as mybir
+
+D, T, I, Q = 512, 1024, 512, 128
+FLOPS = 2 * 2 * D * Q * T
+
+F32 = mybir.dt.float32
+BF16 = mybir.dt.bfloat16
+I32 = mybir.dt.int32
+U32 = mybir.dt.uint32
+U16 = mybir.dt.uint16
+U8 = mybir.dt.uint8
+FP8X4 = mybir.dt.float8_e4m3fn_x4
+ALU = mybir.AluOpType
+ACT = mybir.ActivationFunctionType
+
+P = 128
+PACK = 4
+BANK = 512
+SLOTS = 256
+PER_COL = 16
+STORE = 256
+
+
+def tile_attend_eithertoken_lean_putold_heads_kernel(
+    tc, query, query2, keys_words, keys_scales, lam, old, offs, offs2, offs3, out
+):
+    nc = tc.nc
+    with ExitStack() as ctx:
+        lists = ctx.enter_context(tc.tile_pool(name="lists", bufs=1))
+        sb = ctx.enter_context(tc.tile_pool(name="sb", bufs=1))
+        psum = ctx.enter_context(tc.psum_pool(name="psum", bufs=1))
+
+        key_scales = sb.tile([P, T], U8, name="key_scales", align_bytes=64)
+        nc.vector.memset(key_scales[:].bitcast(I32), 0)
+
+        words = keys_words[0].rearrange("p n t -> p (n t)").bitcast(I32)
+        key_codes = [sb.tile([P, BANK], U32, name="key_codes%d" % h, align_bytes=64) for h in range(2)]
+        raw_a = sb.tile([P, PACK, Q], F32, name="raw_a")
+        raw_b = sb.tile([P, PACK, Q], F32, name="raw_b", tag="raw_b_then_old")
+        nc.sync.dma_start(out=raw_a[:], in_=query.rearrange("(p j) w -> p j w", j=PACK))
+        nc.sync.dma_start(out=key_codes[0][:].bitcast(I32), in_=words[:, 0:BANK])
+        for quad in range(4):
+            nc.sync.dma_start(
+                out=key_scales[32 * quad : 32 * quad + 4, :].bitcast(I32),
+                in_=keys_scales[0, 4 * quad : 4 * quad + 4, :].bitcast(I32),
+            )
+        nc.sync.dma_start(out=raw_b[:], in_=query2.rearrange("(p j) w -> p j w", j=PACK))
+        nc.sync.dma_start(out=key_codes[1][:].bitcast(I32), in_=words[:, BANK:T])
+
+        list_a = lists.tile([P, I // PER_COL], U16, name="list_a")
+        list_b = lists.tile([P, I // PER_COL], U16, name="list_b")
+        list_put = lists.tile([P, I // PER_COL], U16, name="list_put")
+        nc.sync.dma_start(list_a[:], offs)
+        nc.sync.dma_start(list_b[:], offs2)
+        nc.sync.dma_start(list_put[:], offs3)
+        lam_sb = sb.tile([P, 1], F32, name="lam_sb")
+        nc.sync.dma_start(out=lam_sb[:], in_=lam)
+
+        placed = sb.tile([P, T], F32, name="placed")
+        nc.vector.memset(placed[:], 0.0)
+
+        def quantize(raw, name):
+            grouped = sb.tile([P, Q, PACK], BF16, name="grouped_" + name, align_bytes=64)
+            nc.vector.tensor_copy(
+                out=grouped[:].rearrange("p (c i) t -> p c t i", i=4),
+                in_=raw[:].rearrange("p t (c i) -> p c t i", i=4),
+            )
+            codes = sb.tile([P, Q], U32, name="codes_" + name, align_bytes=64)
+            scales = sb.tile([P, Q], U8, name="scales_" + name, align_bytes=64)
+            nc.vector.quantize_mx(
+                out=codes[:].bitcast(FP8X4), scales=scales[:], in_=grouped[:].rearrange("p w j -> p (w j)")
+            )
+            return codes, scales
+
+        def score(codes, scales, c0, c1, name):
+            bank = psum.tile([P, BANK], F32, name="bank_" + name)
+            half = c0 // BANK
+            nc.tensor.matmul_mx(
+                out=bank[:, 0 : c1 - c0],
+                lhsT=codes[:].bitcast(FP8X4),
+                lhsT_scale=scales[:],
+                rhs=key_codes[half][:, c0 - half * BANK : c1 - half * BANK].bitcast(FP8X4),
+                rhs_scale=key_scales[:, c0:c1],
+                start=True,
+                stop=True,
+            )
+            return bank[:, 0 : c1 - c0]
+
+        a_sb = sb.tile([P, T], F32, name="a_sb")
+        b_sb = sb.tile([P, T], F32, name="b_sb")
+        codes_a, scales_a = quantize(raw_a, "a")
+        codes_b, scales_b = quantize(raw_b, "b")
+
+        old_sb = sb.tile([P, T], F32, name="old_sb", tag="raw_b_then_old")
+        nc.sync.dma_start(out=old_sb[:], in_=old)
+
+        nc.scalar.copy(out=a_sb[:, 0:512], in_=score(codes_a, scales_a, 0, 512, "a0"))
+        nc.vector.tensor_copy(out=a_sb[:, 512:768], in_=score(codes_a, scales_a, 512, 768, "a1"))
+        nc.scalar.copy(out=a_sb[:, 768:1024], in_=score(codes_a, scales_a, 768, 1024, "a2"))
+        nc.vector.tensor_copy(out=b_sb[:, 0:512], in_=score(codes_b, scales_b, 0, 512, "b0"))
+        nc.vector.tensor_copy(out=b_sb[:, 512:768], in_=score(codes_b, scales_b, 512, 768, "b1"))
+        nc.vector.tensor_copy(out=b_sb[:, 768:1024], in_=score(codes_b, scales_b, 768, 1024, "b2"))
+
+        neg_lam = sb.tile([P, 1], F32, name="neg_lam")
+        nc.vector.tensor_scalar(out=neg_lam[:], in0=lam_sb[:], scalar1=-1.0, scalar2=None, op0=ALU.mult)
+
+        cols = SLOTS // PER_COL
+        a_pick = sb.tile([P, I], F32, name="a_pick")
+        diff = sb.tile([P, I], F32, name="diff")
+        th = sb.tile([P, I], F32, name="th")
+        abs_th = sb.tile([P, I], F32, name="abs_th")
+        larger = sb.tile([P, I], F32, name="larger")
+        neg_larger = sb.tile([P, I], F32, name="neg_larger")
+        log_share = sb.tile([P, I], F32, name="log_share")
+        parts = [(slice(k * SLOTS, (k + 1) * SLOTS), slice(k * cols, (k + 1) * cols)) for k in range(I // SLOTS)]
+
+        for slots, lc in parts:
+            nc.scalar.activation(out=a_pick[:, slots], in_=a_sb[:].indirect(list_a[:, lc]), func=ACT.Copy)
+        for slots, lc in parts:
+            nc.vector.tensor_tensor(
+                out=diff[:, slots], in0=b_sb[:].indirect(list_b[:, lc]), in1=a_pick[:, slots], op=ALU.subtract
+            )
+        for slots, lc in parts:
+            nc.scalar.activation(out=th[:, slots], in_=diff[:, slots], func=ACT.Tanh, scale=0.5)
+        nc.vector.scalar_tensor_tensor(
+            out=larger[:], in0=diff[:], scalar=0.0, in1=a_pick[:], op0=ALU.max, op1=ALU.add
+        )
+        nc.vector.scalar_tensor_tensor(out=abs_th[:], in0=th[:], scalar=-1.0, in1=th[:], op0=ALU.mult, op1=ALU.max)
+        nc.vector.tensor_scalar(out=neg_larger[:], in0=larger[:], scalar1=-1.0, scalar2=None, op0=ALU.mult)
+        for slots, lc in parts:
+            nc.scalar.activation(out=log_share[:, slots], in_=abs_th[:, slots], func=ACT.Ln, scale=0.5, bias=0.5)
+        for slots, lc in parts:
+            nc.vector.tensor_tensor(
+                out=placed[:].indirect(list_put[:, lc]), in0=neg_larger[:, slots], in1=log_share[:, slots], op=ALU.add
+            )
+
+        result = sb.tile([P, T], F32, name="result")
+        for c0 in range(0, T, STORE):
+            span = slice(c0, c0 + STORE)
+            nc.vector.scalar_tensor_tensor(
+                out=result[:, span], in0=placed[:, span], scalar=neg_lam[:], in1=old_sb[:, span],
+                op0=ALU.mult, op1=ALU.add,
+            )
+            nc.sync.dma_start(out=out[:, span], in_=result[:, span])

@@ -21,6 +21,7 @@ BANK = 512
 SLOTS = 256
 PER_COL = 16
 STORE = 256
+PIECE = 256
 
 
 def tile_attend_eithertoken_lean_putold_heads_kernel(
@@ -96,12 +97,10 @@ def tile_attend_eithertoken_lean_putold_heads_kernel(
         old_sb = sb.tile([P, T], F32, name="old_sb", tag="raw_b_then_old")
         nc.sync.dma_start(out=old_sb[:], in_=old)
 
-        nc.scalar.copy(out=a_sb[:, 0:512], in_=score(codes_a, scales_a, 0, 512, "a0"))
-        nc.vector.tensor_copy(out=a_sb[:, 512:768], in_=score(codes_a, scales_a, 512, 768, "a1"))
-        nc.scalar.copy(out=a_sb[:, 768:1024], in_=score(codes_a, scales_a, 768, 1024, "a2"))
-        nc.vector.tensor_copy(out=b_sb[:, 0:512], in_=score(codes_b, scales_b, 0, 512, "b0"))
-        nc.vector.tensor_copy(out=b_sb[:, 512:768], in_=score(codes_b, scales_b, 512, 768, "b1"))
-        nc.vector.tensor_copy(out=b_sb[:, 768:1024], in_=score(codes_b, scales_b, 768, 1024, "b2"))
+        for c0 in range(0, T, PIECE):
+            nc.scalar.copy(out=a_sb[:, c0 : c0 + PIECE], in_=score(codes_a, scales_a, c0, c0 + PIECE, "a%d" % c0))
+        for c0 in range(0, T, PIECE):
+            nc.scalar.copy(out=b_sb[:, c0 : c0 + PIECE], in_=score(codes_b, scales_b, c0, c0 + PIECE, "b%d" % c0))
 
         neg_lam = sb.tile([P, 1], F32, name="neg_lam")
         nc.vector.tensor_scalar(out=neg_lam[:], in0=lam_sb[:], scalar1=-1.0, scalar2=None, op0=ALU.mult)
@@ -117,11 +116,14 @@ def tile_attend_eithertoken_lean_putold_heads_kernel(
         parts = [(slice(k * SLOTS, (k + 1) * SLOTS), slice(k * cols, (k + 1) * cols)) for k in range(I // SLOTS)]
 
         for slots, lc in parts:
-            nc.scalar.activation(out=a_pick[:, slots], in_=a_sb[:].indirect(list_a[:, lc]), func=ACT.Copy)
-        for slots, lc in parts:
-            nc.vector.tensor_tensor(
-                out=diff[:, slots], in0=b_sb[:].indirect(list_b[:, lc]), in1=a_pick[:, slots], op=ALU.subtract
-            )
+            nc.vector.tensor_copy(out=a_pick[:, slots], in_=a_sb[:].indirect(list_a[:, lc]))
+        (slots0, lc0), (slots1, lc1) = parts
+        b_pick = sb.tile([P, SLOTS], F32, name="b_pick")
+        nc.vector.tensor_tensor(
+            out=diff[:, slots0], in0=b_sb[:].indirect(list_b[:, lc0]), in1=a_pick[:, slots0], op=ALU.subtract
+        )
+        nc.scalar.activation(out=b_pick[:], in_=b_sb[:].indirect(list_b[:, lc1]), func=ACT.Copy)
+        nc.vector.tensor_tensor(out=diff[:, slots1], in0=b_pick[:], in1=a_pick[:, slots1], op=ALU.subtract)
         for slots, lc in parts:
             nc.scalar.activation(out=th[:, slots], in_=diff[:, slots], func=ACT.Tanh, scale=0.5)
         nc.vector.scalar_tensor_tensor(

from contextlib import ExitStack

import concourse.mybir as mybir

D, T, I, Q = 512, 1024, 512, 128
FLOPS = 2 * 2 * D * Q * T

F32 = mybir.dt.float32
BF16 = mybir.dt.bfloat16
I32 = mybir.dt.int32
U32 = mybir.dt.uint32
U16 = mybir.dt.uint16
U8 = mybir.dt.uint8
FP8X4 = mybir.dt.float8_e4m3fn_x4
ALU = mybir.AluOpType
ACT = mybir.ActivationFunctionType

P = 128
PACK = 4
BANK = 512
SLOTS = 256
PER_COL = 16
STORE = 256
PIECE = 256


def tile_attend_eithertoken_lean_putold_heads_kernel(
    tc, query, query2, keys_words, keys_scales, lam, old, offs, offs2, offs3, out
):
    nc = tc.nc
    with ExitStack() as ctx:
        lists = ctx.enter_context(tc.tile_pool(name="lists", bufs=1))
        sb = ctx.enter_context(tc.tile_pool(name="sb", bufs=1))
        psum = ctx.enter_context(tc.psum_pool(name="psum", bufs=1))

        key_scales = sb.tile([P, T], U8, name="key_scales", align_bytes=64)
        nc.vector.memset(key_scales[:].bitcast(I32), 0)

        words = keys_words[0].rearrange("p n t -> p (n t)").bitcast(I32)
        key_codes = [sb.tile([P, BANK], U32, name="key_codes%d" % h, align_bytes=64) for h in range(2)]
        raw_a = sb.tile([P, PACK, Q], F32, name="raw_a")
        raw_b = sb.tile([P, PACK, Q], F32, name="raw_b", tag="raw_b_then_old")
        nc.sync.dma_start(out=raw_a[:], in_=query.rearrange("(p j) w -> p j w", j=PACK))
        nc.sync.dma_start(out=key_codes[0][:].bitcast(I32), in_=words[:, 0:BANK])
        for quad in range(4):
            nc.sync.dma_start(
                out=key_scales[32 * quad : 32 * quad + 4, :].bitcast(I32),
                in_=keys_scales[0, 4 * quad : 4 * quad + 4, :].bitcast(I32),
            )
        nc.sync.dma_start(out=raw_b[:], in_=query2.rearrange("(p j) w -> p j w", j=PACK))
        nc.sync.dma_start(out=key_codes[1][:].bitcast(I32), in_=words[:, BANK:T])

        list_a = lists.tile([P, I // PER_COL], U16, name="list_a")
        list_b = lists.tile([P, I // PER_COL], U16, name="list_b")
        list_put = lists.tile([P, I // PER_COL], U16, name="list_put")
        nc.sync.dma_start(list_a[:], offs)
        nc.sync.dma_start(list_b[:], offs2)
        nc.sync.dma_start(list_put[:], offs3)
        lam_sb = sb.tile([P, 1], F32, name="lam_sb")
        nc.sync.dma_start(out=lam_sb[:], in_=lam)

        placed = sb.tile([P, T], F32, name="placed")
        nc.vector.memset(placed[:], 0.0)

        def quantize(raw, name):
            grouped = sb.tile([P, Q, PACK], BF16, name="grouped_" + name, align_bytes=64)
            nc.vector.tensor_copy(
                out=grouped[:].rearrange("p (c i) t -> p c t i", i=4),
                in_=raw[:].rearrange("p t (c i) -> p c t i", i=4),
            )
            codes = sb.tile([P, Q], U32, name="codes_" + name, align_bytes=64)
            scales = sb.tile([P, Q], U8, name="scales_" + name, align_bytes=64)
            nc.vector.quantize_mx(
                out=codes[:].bitcast(FP8X4), scales=scales[:], in_=grouped[:].rearrange("p w j -> p (w j)")
            )
            return codes, scales

        def score(codes, scales, c0, c1, name):
            bank = psum.tile([P, BANK], F32, name="bank_" + name)
            half = c0 // BANK
            nc.tensor.matmul_mx(
                out=bank[:, 0 : c1 - c0],
                lhsT=codes[:].bitcast(FP8X4),
                lhsT_scale=scales[:],
                rhs=key_codes[half][:, c0 - half * BANK : c1 - half * BANK].bitcast(FP8X4),
                rhs_scale=key_scales[:, c0:c1],
                start=True,
                stop=True,
            )
            return bank[:, 0 : c1 - c0]

        a_sb = sb.tile([P, T], F32, name="a_sb")
        b_sb = sb.tile([P, T], F32, name="b_sb")
        codes_a, scales_a = quantize(raw_a, "a")
        codes_b, scales_b = quantize(raw_b, "b")

        old_sb = sb.tile([P, T], F32, name="old_sb", tag="raw_b_then_old")
        nc.sync.dma_start(out=old_sb[:], in_=old)

        for c0 in range(0, T, PIECE):
            nc.scalar.copy(out=a_sb[:, c0 : c0 + PIECE], in_=score(codes_a, scales_a, c0, c0 + PIECE, "a%d" % c0))
        for c0 in range(0, T, PIECE):
            nc.scalar.copy(out=b_sb[:, c0 : c0 + PIECE], in_=score(codes_b, scales_b, c0, c0 + PIECE, "b%d" % c0))

        neg_lam = sb.tile([P, 1], F32, name="neg_lam")
        nc.vector.tensor_scalar(out=neg_lam[:], in0=lam_sb[:], scalar1=-1.0, scalar2=None, op0=ALU.mult)

        cols = SLOTS // PER_COL
        a_pick = sb.tile([P, I], F32, name="a_pick")
        diff = sb.tile([P, I], F32, name="diff")
        th = sb.tile([P, I], F32, name="th")
        abs_th = sb.tile([P, I], F32, name="abs_th")
        larger = sb.tile([P, I], F32, name="larger")
        neg_larger = sb.tile([P, I], F32, name="neg_larger")
        log_share = sb.tile([P, I], F32, name="log_share")
        parts = [(slice(k * SLOTS, (k + 1) * SLOTS), slice(k * cols, (k + 1) * cols)) for k in range(I // SLOTS)]

        for slots, lc in parts:
            nc.vector.tensor_copy(out=a_pick[:, slots], in_=a_sb[:].indirect(list_a[:, lc]))
        (slots0, lc0), (slots1, lc1) = parts
        b_pick = sb.tile([P, SLOTS], F32, name="b_pick")
        nc.vector.tensor_tensor(
            out=diff[:, slots0], in0=b_sb[:].indirect(list_b[:, lc0]), in1=a_pick[:, slots0], op=ALU.subtract
        )
        nc.scalar.activation(out=b_pick[:], in_=b_sb[:].indirect(list_b[:, lc1]), func=ACT.Copy)
        nc.vector.tensor_tensor(out=diff[:, slots1], in0=b_pick[:], in1=a_pick[:, slots1], op=ALU.subtract)
        for slots, lc in parts:
            nc.scalar.activation(out=th[:, slots], in_=diff[:, slots], func=ACT.Tanh, scale=0.5)
        nc.vector.scalar_tensor_tensor(
            out=larger[:], in0=diff[:], scalar=0.0, in1=a_pick[:], op0=ALU.max, op1=ALU.add
        )
        nc.vector.scalar_tensor_tensor(out=abs_th[:], in0=th[:], scalar=-1.0, in1=th[:], op0=ALU.mult, op1=ALU.max)
        nc.vector.tensor_scalar(out=neg_larger[:], in0=larger[:], scalar1=-1.0, scalar2=None, op0=ALU.mult)
        for slots, lc in parts:
            nc.scalar.activation(out=log_share[:, slots], in_=abs_th[:, slots], func=ACT.Ln, scale=0.5, bias=0.5)
        for slots, lc in parts:
            nc.vector.tensor_tensor(
                out=placed[:].indirect(list_put[:, lc]), in0=neg_larger[:, slots], in1=log_share[:, slots], op=ALU.add
            )

        result = sb.tile([P, T], F32, name="result")
        for c0 in range(0, T, STORE):
            span = slice(c0, c0 + STORE)
            nc.vector.scalar_tensor_tensor(
                out=result[:, span], in0=placed[:, span], scalar=neg_lam[:], in1=old_sb[:, span],
                op0=ALU.mult, op1=ALU.add,
            )
            nc.sync.dma_start(out=out[:, span], in_=result[:, span])
